import numpy as np
import ml_dtypes


def mxq(x, axis, fmt="e4m3"):
    dtype, down = {"e4m3": (ml_dtypes.float8_e4m3fn, 7), "e5m2": (ml_dtypes.float8_e5m2, 14)}[fmt]
    v = np.moveaxis(np.asarray(x, np.float32).astype(ml_dtypes.bfloat16).astype(np.float64), axis, -1)
    blocks = v.reshape(v.shape[:-1] + (-1, 32))
    amax = np.abs(blocks).max(-1, keepdims=True)
    byte = np.maximum(np.where(amax > 0, np.frexp(amax)[1] - 1 + 127, 0) - down, 1)
    scale = np.exp2(byte - 127.0)
    codes = (blocks / scale).astype(np.float32).astype(dtype).astype(np.float64)
    return np.moveaxis((codes * scale).reshape(v.shape), -1, axis)


WIDE = False


def mx_kscale(k):
    if not WIDE:
        return np.ones(k)
    levels = np.array([10, -10, 5, -5, 0])
    if k % 512:
        return np.exp2(np.random.permutation(np.resize(levels, k // 32))).repeat(32)
    a = np.empty((k // 512, 16))
    for p in range(k // 512):
        a[p, :8] = np.random.permutation(np.resize(levels, 8))
        for g in range(8):
            far = levels[np.abs(levels - a[p, g]) >= 10]
            a[p, g + 8] = far[np.random.randint(len(far))]
    return np.exp2(a.ravel()).repeat(32)


def f64(x):
    return np.asarray(x).astype(np.float64)


def striped(idx):
    return np.tile(idx.reshape(-1, 16).T, (8, 1)).astype(np.uint16)


def unstriped(offs):
    return offs[:16].T.reshape(-1).astype(np.int64)


def pack_weight(w):
    k, n = w.shape
    w = f64(np.asarray(w, np.float32).astype(ml_dtypes.bfloat16)).reshape(k // 32, 32, n)
    amax = np.abs(w).max(1)
    byte = np.clip(np.where(amax > 0, np.frexp(amax)[1] - 1 + 127 - 7, 1), 1, 254)
    scaled = (w * np.exp2(127.0 - byte)[:, None, :]).reshape(k, n).astype(np.float32)
    words = np.ascontiguousarray(scaled.reshape(k // 512, 128, 4, n).transpose(0, 1, 3, 2)).astype(ml_dtypes.float8_e4m3fn).view(np.uint8)
    return words, np.ascontiguousarray(byte.astype(np.uint8).reshape(k // 512, 16, n))


def unpack_weight(words, scales):
    g, p, n, _ = words.shape
    vals = np.ascontiguousarray(words).view(ml_dtypes.float8_e4m3fn).astype(np.float64) * np.repeat(np.exp2(scales.astype(np.float64) - 127.0), 8, axis=1)[..., None]
    return vals.transpose(0, 1, 3, 2).reshape(g * 512, n)


E2M1 = np.array([0.0, 0.5, 1.0, 1.5, 2.0, 3.0, 4.0, 6.0, -0.0, -0.5, -1.0, -1.5, -2.0, -3.0, -4.0, -6.0])


def pack_fp4(w):
    k, n = w.shape
    w = f64(np.asarray(w, np.float32).astype(ml_dtypes.bfloat16)).reshape(k // 32, 32, n)
    amax = np.abs(w).max(1)
    mant, ex = np.frexp(amax / 6.0)
    byte = np.clip(np.where(amax > 0, np.where(mant > 0.5, ex, ex - 1) + 127, 1), 1, 254)
    scaled = (w * np.exp2(127.0 - byte)[:, None, :]).reshape(k, n).astype(np.float32)
    c = np.ascontiguousarray(scaled.reshape(k // 512, 128, 4, n).transpose(0, 1, 3, 2)).astype(ml_dtypes.float4_e2m1fn).view(np.uint8) & 0xF
    words = (c[..., 0::2] | (c[..., 1::2] << 4)).reshape(k // 512, 128, 2 * n)
    return np.ascontiguousarray(words), np.ascontiguousarray(byte.astype(np.uint8).reshape(k // 512, 16, n))


def unpack_fp4(words, scales):
    g, _, n = scales.shape
    words = np.ascontiguousarray(words).reshape(g, 128, n, 2)
    nib = np.empty((g, 128, n, 4), np.uint8)
    nib[..., 0::2] = words & 0xF
    nib[..., 1::2] = words >> 4
    vals = E2M1[nib] * np.repeat(np.exp2(scales.astype(np.float64) - 127.0), 8, axis=1)[..., None]
    return vals.transpose(0, 1, 3, 2).reshape(g * 512, n)


def relu(v):
    return np.maximum(v, 0.0)

def planes(y):
    n, m = y.shape
    v = y.astype(np.float32).astype(ml_dtypes.bfloat16).astype(np.float64).reshape(n // 32, 32, m)
    top = np.abs(v).max(1)
    byte = np.clip(np.where(top > 0, np.frexp(top)[1] - 1 + 127 - 7, 1), 1, 254)
    codes = (v * np.exp2(127.0 - byte)[:, None, :]).reshape(n, m).astype(np.float32).astype(ml_dtypes.float8_e4m3fn).view(np.uint8)
    words = codes.reshape(n // 512, 128, 4, m).transpose(0, 1, 3, 2)
    return np.ascontiguousarray(words), np.ascontiguousarray(byte.astype(np.uint8).reshape(n // 512, 16, m))


K, T, S, H, W, C, U = 512, 2048, 512, 512, 2048, 512, 1024


def setup_inputs():
    n = np.random.standard_normal
    s = mx_kscale(K)[:, None]
    packed_xT = pack_weight(n((K, T)) * s)
    packed_w1 = pack_fp4(n((K, H)) / np.sqrt(K) / s)
    return {
        "x_words": packed_xT[0],
        "x_scales": packed_xT[1],
        "w1_words": packed_w1[0],
        "w1_scales": packed_w1[1],
        "gs": (np.random.uniform(0.5, 1.5, (K, 1)) / s).astype(np.float32),
        "offs": striped(np.random.permutation(T)[:S]),
        "n1": striped(np.random.randint(0, S, W)),
        "cand": striped(np.random.permutation(T)[:C]),
        "n2": striped(np.random.permutation(U)[:S]),
        "n3": striped(np.random.permutation(S)),
    }


def reference(x_words, x_scales, w1_words, w1_scales, gs, offs, n1, cand, n2, n3):
    x_cand = unpack_weight(x_words, x_scales)[:, unstriped(cand)]
    xq = unpack_weight(x_words, x_scales)[:, unstriped(offs)]
    y = unpack_fp4(w1_words, w1_scales).T @ xq
    mb = y[:, unstriped(n1)]
    sq = (mb) ** 2
    qs = sq.reshape(H, S, 4).sum(axis=2)
    z = f64(gs) * (y / np.sqrt(qs + 0.5))
    s = 0.0625 * ((x_cand.T @ mxq(z, 0, "e4m3")))
    nw = s - (relu(s[:, unstriped(n3)]))
    out = np.zeros((C, U))
    out[:, unstriped(n2)] = nw
    return (out,) + planes(out)

@@ -1,0 +1,269 @@
+from contextlib import ExitStack
+
+import concourse.mybir as mybir
+
+F32 = mybir.dt.float32
+BF16 = mybir.dt.bfloat16
+I32 = mybir.dt.int32
+U32 = mybir.dt.uint32
+U16 = mybir.dt.uint16
+U8 = mybir.dt.uint8
+FP8X4 = mybir.dt.float8_e4m3fn_x4
+FP4X4 = mybir.dt.float4_e2m1fn_x4
+ALU = mybir.AluOpType
+ACT = mybir.ActivationFunctionType
+AX = mybir.AxisListType
+
+P = 128
+PACK = 4
+K, T, S, H, C, U = 512, 2048, 512, 512, 512, 1024
+MEMBERS = 4
+CHUNKS = [128, 128, 128, 64, 64]
+SPARE = 16
+SCALAR_SQUARES = 4
+HALF = S // 2
+FLOPS = 2 * K * H * S + 2 * H * C * S
+
+
+def tile_picked_candgvarpagez_none_po_kernel(
+    tc, x_words, x_scales, w1_words, w1_scales, gs, offs, n1, cand, n2, n3, out_0, out_1, out_2
+):
+    nc = tc.nc
+    with ExitStack() as ctx:
+        keep = ctx.enter_context(tc.tile_pool(name="keep", bufs=1))
+        ring = ctx.enter_context(tc.tile_pool(name="ring", bufs=2))
+        psum = ctx.enter_context(tc.psum_pool(name="psum", bufs=1))
+
+        offs_t = keep.tile([P, S // 16], U16, name="offs_t")
+        n1_t = keep.tile([P, S * MEMBERS // 16], U16, name="n1_t")
+        cand_t = keep.tile([P, C // 16], U16, name="cand_t")
+        n2_t = keep.tile([P, S // 16], U16, name="n2_t")
+        n3_t = keep.tile([P, S // 16], U16, name="n3_t")
+
+        xw = keep.tile([P, T], I32, name="xw", align_bytes=64)
+        xs = keep.tile([P, T], U8, name="xs", align_bytes=64)
+        ww = keep.tile([P, 2 * H], U8, name="ww", align_bytes=64)
+        ws = keep.tile([P, H], U8, name="ws", align_bytes=64)
+        gs_t = keep.tile([P, PACK], F32, name="gs_t")
+
+        nc.vector.memset(xs[:].bitcast(I32), 0)
+        nc.gpsimd.memset(ws[:].bitcast(I32), 0)
+
+        def load_scale_rows(engine, tile, scales, q):
+            engine.dma_start(tile[32 * q : 32 * q + 4, :].bitcast(I32), scales[0, 4 * q : 4 * q + 4, :].bitcast(I32))
+
+        nc.sync.dma_start(offs_t[:], offs)
+        nc.sync.dma_start(xw[:], x_words[0].rearrange("p c r -> p (c r)").bitcast(I32))
+        nc.sync.dma_start(ww[:].bitcast(I32), w1_words[0].bitcast(I32))
+        for q in range(4):
+            load_scale_rows(nc.sync, xs, x_scales, q)
+        for q in range(4):
+            load_scale_rows(nc.sync if q < 2 else nc.gpsimd, ws, w1_scales, q)
+        nc.sync.dma_start(gs_t[:], gs.rearrange("(p t) o -> p (t o)", t=PACK))
+        nc.sync.dma_start(n1_t[:], n1)
+        nc.sync.dma_start(cand_t[:], cand)
+        nc.sync.dma_start(n3_t[:], n3)
+        nc.sync.dma_start(n2_t[:], n2)
+
+        ysq = [keep.tile([P, S + SPARE], F32, name="ysq%d" % t) for t in range(PACK)]
+        page = [keep.tile([P, U], F32, name="page%d" % t) for t in range(PACK)]
+        for t in range(PACK):
+            nc.gpsimd.memset(ysq[t][:, S:], 0.0)
+        for t in range(PACK):
+            nc.gpsimd.memset(page[t][:], 0.0)
+
+        ww_d = keep.tile([P, 2 * H], U8, name="ww_d", align_bytes=64)
+        ws_d = keep.tile([P, H], U8, name="ws_d", align_bytes=64)
+        nc.vector.tensor_copy(
+            ww_d[:].rearrange("p (t m b) -> p m t b", t=PACK, b=2), ww[:].rearrange("p (m t b) -> p m t b", t=PACK, b=2)
+        )
+        nc.vector.tensor_copy(
+            ws_d[:].rearrange("p (t m) -> p m t", t=PACK), ws[:].rearrange("p (m t) -> p m t", t=PACK)
+        )
+
+        xq_s = keep.tile([P, S], U8, name="xq_s", align_bytes=64)
+        nc.vector.tensor_copy(xq_s[:], xs[:].indirect(offs_t[:]))
+        xq_w = keep.tile([P, S], U32, name="xq_w", align_bytes=64)
+        for h in range(2):
+            nc.vector.tensor_copy(
+                xq_w[:, h * HALF : (h + 1) * HALF],
+                xw[:].bitcast(U32).indirect(offs_t[:, h * HALF // 16 : (h + 1) * HALF // 16]),
+            )
+
+        yg = keep.tile([P, PACK, S], F32, name="yg")
+
+        def project(t, j0, n):
+            cols = slice(j0, j0 + n)
+            y_ps = psum.tile([P, n], F32, name="y_ps%d_%d" % (t, j0))
+            nc.tensor.matmul_mx(
+                out=y_ps[:],
+                lhsT=ww_d[:, 2 * P * t : 2 * P * (t + 1)].bitcast(FP4X4),
+                lhsT_scale=ws_d[:, P * t : P * (t + 1)],
+                rhs=xq_w[:, cols].bitcast(FP8X4),
+                rhs_scale=xq_s[:, cols],
+                start=True,
+                stop=True,
+            )
+            if t < SCALAR_SQUARES:
+                nc.scalar.activation(ysq[t][:, cols], y_ps[:], ACT.Square)
+                y_of.append((t, cols, y_ps))
+            else:
+                y_sb = ring.tile([P, n], F32, name="y_sb", bufs=PACK - SCALAR_SQUARES)
+                nc.vector.tensor_copy(y_sb[:], y_ps[:])
+                nc.vector.tensor_tensor(ysq[t][:, cols], y_ps[:], y_sb[:], ALU.mult)
+                y_of.append((t, cols, y_sb))
+
+        def weigh(tiles):
+            for t, cols, y in y_of:
+                if t in tiles:
+                    nc.vector.tensor_scalar(yg[:, t, cols], y[:], gs_t[:, t : t + 1], None, ALU.mult)
+
+        y_of = []
+        project(0, 0, HALF)
+        project(0, HALF, HALF)
+        for t in range(1, PACK):
+            project(t, 0, S)
+
+        xc_w = keep.tile([P, C], U32, name="xc_w", align_bytes=64)
+        xc_s = keep.tile([P, C], U8, name="xc_s", align_bytes=64)
+        xc_wd = keep.tile([P, C], U32, name="xc_wd", align_bytes=64)
+        xc_sd = keep.tile([P, C], U8, name="xc_sd", align_bytes=64)
+
+        def cand_words():
+            nc.vector.tensor_copy(xc_w[:], xw[:].bitcast(U32).indirect(cand_t[:]))
+
+        def cand_scales():
+            nc.vector.tensor_copy(xc_s[:], xs[:].indirect(cand_t[:]))
+
+        def cand_deal():
+            nc.vector.tensor_copy(
+                xc_wd[:].bitcast(I32).rearrange("p (t m) -> p t m", t=PACK),
+                xc_w[:].bitcast(I32).rearrange("p (m t) -> p t m", t=PACK),
+            )
+            nc.vector.tensor_copy(
+                xc_sd[:].rearrange("p (t m) -> p m t", t=PACK), xc_s[:].rearrange("p (m t) -> p m t", t=PACK)
+            )
+
+        s_sb = keep.tile([P, PACK, S], F32, name="s_sb")
+        starts = [sum(CHUNKS[:c]) for c in range(len(CHUNKS))]
+        last = len(CHUNKS) - 1
+        mb_of, qs_of, r_of, s_ps_of = {}, {}, {}, {}
+
+        def fetch(c, t):
+            n = CHUNKS[c]
+            if t == 0:
+                qs_of[c] = ring.tile([P, PACK, n], F32, name="qs")
+                mb_of[c, 0] = ring.tile([P, n * MEMBERS], F32, name="mb_first", bufs=1)[:]
+            if t == 1:
+                rest = ring.tile([P, PACK - 1, n * MEMBERS], F32, name="mb_rest", bufs=1)
+                for u in range(1, PACK):
+                    mb_of[c, u] = rest[:, u - 1, :]
+            mb = mb_of[c, t]
+            lst = slice(starts[c] * MEMBERS // 16, (starts[c] + n) * MEMBERS // 16)
+            nc.scalar.activation(mb, ysq[t][:].indirect(n1_t[:, lst]), ACT.Copy)
+            nc.vector.tensor_reduce(qs_of[c][:, t, :], mb.rearrange("p (j m) -> p j m", m=MEMBERS), AX.X, ALU.add)
+
+        def root(c):
+            r_of[c] = ring.tile([P, PACK, CHUNKS[c]], F32, name="r")
+            nc.scalar.activation(r_of[c][:], qs_of[c][:], ACT.Abs_reciprocal_sqrt, bias=0.5)
+
+        def score(c):
+            n = CHUNKS[c]
+            cols = slice(starts[c], starts[c] + n)
+            zb = ring.tile([P, n * PACK], BF16, name="zb", align_bytes=64)
+            nc.vector.tensor_tensor(
+                zb[:].rearrange("p (g i t) -> p g t i", i=4, t=PACK),
+                yg[:, :, cols].rearrange("p t (g i) -> p g t i", i=4),
+                r_of[c][:].rearrange("p t (g i) -> p g t i", i=4),
+                ALU.mult,
+            )
+            z_w = ring.tile([P, n], U32, name="z_w", align_bytes=64)
+            z_s = ring.tile([P, n], U8, name="z_s", align_bytes=64)
+            nc.vector.quantize_mx(out=z_w[:].bitcast(FP8X4), scales=z_s[:], in_=zb[:])
+            s_ps = psum.tile([P, PACK, n], F32, name="s_ps", bufs=2)
+            for t in range(PACK):
+                nc.tensor.matmul_mx(
+                    out=s_ps[:, t, :],
+                    lhsT=xc_wd[:, P * t : P * (t + 1)].bitcast(FP8X4),
+                    lhsT_scale=xc_sd[:, P * t : P * (t + 1)],
+                    rhs=z_w[:].bitcast(FP8X4),
+                    rhs_scale=z_s[:],
+                    start=True,
+                    stop=True,
+                )
+            s_ps_of[c] = s_ps
+
+        def copy_s(c, tiles):
+            cols = slice(starts[c], starts[c] + CHUNKS[c])
+            nc.vector.tensor_scalar(s_sb[:, tiles, cols], s_ps_of[c][:, tiles, :], -0.0625, None, ALU.mult)
+
+        weigh((0, 1, 2, 3))
+        cand_words()
+        fetch(0, 0)
+        cand_scales()
+        fetch(0, 1)
+        cand_deal()
+        fetch(0, 2)
+        fetch(0, 3)
+        for c in range(1, len(CHUNKS)):
+            fetch(c, 0)
+            root(c - 1)
+            score(c - 1)
+            fetch(c, 1)
+            copy_s(c - 1, slice(0, PACK))
+            fetch(c, 2)
+            fetch(c, 3)
+        root(last)
+        score(last)
+        copy_s(last, slice(0, 1))
+
+        out_rows = out_0.rearrange("(p t) u -> p t u", t=PACK)
+
+        def put(t, j0, n, final=False):
+            nw = ring.tile([P, n], F32, name="nw", bufs=8)
+            lst = slice(j0 // 16, (j0 + n) // 16)
+            if final:
+                got = keep.tile([P, n], F32, name="got_final", tag="rounded", align_bytes=64)
+            else:
+                got = ring.tile([P, n], F32, name="got", bufs=3)
+            nc.vector.tensor_copy(got[:], s_sb[:, t, :].indirect(n3_t[:, lst]))
+            nc.vector.scalar_tensor_tensor(nw[:], got[:], 0.0, s_sb[:, t, j0 : j0 + n], ALU.min, ALU.subtract)
+            nc.scalar.activation(page[t][:].indirect(n2_t[:, lst]), nw[:], ACT.Copy)
+
+        put(0, 0, 128)
+        copy_s(last, slice(1, PACK))
+        put(1, 0, 256)
+        put(0, 128, 384)
+        put(1, 256, 256)
+        put(2, 0, 256)
+        put(3, 0, 128)
+        put(2, 256, 256)
+        put(3, 128, 384, final=True)
+
+        rounded = keep.tile([P, U * PACK], BF16, name="rounded", tag="rounded", align_bytes=64)
+
+        def round_page(t, h):
+            cols = slice(h * U // 2, (h + 1) * U // 2)
+            nc.vector.tensor_copy(rounded[:].rearrange("p (u t) -> p u t", t=PACK)[:, cols, t], page[t][:, cols])
+
+        for t in range(PACK):
+            nc.sync.dma_start(out_rows[:, t, :], page[t][:])
+            if t < PACK - 1:
+                round_page(t, 0)
+                round_page(t, 1)
+
+        o_w = keep.tile([P, U], U32, name="o_w", align_bytes=64)
+        o_s = keep.tile([P, U], U8, name="o_s", align_bytes=64)
+        words_out = out_1[0].rearrange("p c r -> p (c r)").bitcast(I32)
+        for h in range(2):
+            round_page(PACK - 1, h)
+        for h in range(2):
+            cols = slice(h * U // 2, (h + 1) * U // 2)
+            nc.vector.quantize_mx(
+                out=o_w[:, cols].bitcast(FP8X4), scales=o_s[:, cols], in_=rounded[:, h * 2 * U : (h + 1) * 2 * U]
+            )
+            nc.sync.dma_start(words_out[:, cols], o_w[:, cols].bitcast(I32))
+        for q in range(4):
+            (nc.scalar if q < 3 else nc.sync).dma_start(
+                out_2[0, 4 * q : 4 * q + 4, :].bitcast(I32), o_s[32 * q : 32 * q + 4, :].bitcast(I32)
+            )

@@ -20,7 +20,6 @@ K, T, S, H, C, U = 512, 2048, 512, 512, 512, 1024
 MEMBERS = 4
 CHUNKS = [128, 128, 128, 64, 64]
 SPARE = 16
-SCALAR_SQUARES = 4
 HALF = S // 2
 FLOPS = 2 * K * H * S + 2 * H * C * S
 
@@ -54,41 +53,48 @@ def tile_picked_candgvarpagez_none_po_kernel(
 
         nc.sync.dma_start(offs_t[:], offs)
         nc.sync.dma_start(xw[:], x_words[0].rearrange("p c r -> p (c r)").bitcast(I32))
-        nc.sync.dma_start(ww[:].bitcast(I32), w1_words[0].bitcast(I32))
+        nc.scalar.dma_start(ww[:].bitcast(I32), w1_words[0].bitcast(I32))
         for q in range(4):
-            load_scale_rows(nc.sync, xs, x_scales, q)
+            load_scale_rows(nc.scalar, xs, x_scales, q)
         for q in range(4):
-            load_scale_rows(nc.sync if q < 2 else nc.gpsimd, ws, w1_scales, q)
-        nc.sync.dma_start(gs_t[:], gs.rearrange("(p t) o -> p (t o)", t=PACK))
+            load_scale_rows(nc.scalar if q < 2 else nc.gpsimd, ws, w1_scales, q)
         nc.sync.dma_start(n1_t[:], n1)
         nc.sync.dma_start(cand_t[:], cand)
+        nc.sync.dma_start(gs_t[:], gs.rearrange("(p t) o -> p (t o)", t=PACK))
         nc.sync.dma_start(n3_t[:], n3)
         nc.sync.dma_start(n2_t[:], n2)
 
         ysq = [keep.tile([P, S + SPARE], F32, name="ysq%d" % t) for t in range(PACK)]
-        page = [keep.tile([P, U], F32, name="page%d" % t) for t in range(PACK)]
         for t in range(PACK):
             nc.gpsimd.memset(ysq[t][:, S:], 0.0)
-        for t in range(PACK):
-            nc.gpsimd.memset(page[t][:], 0.0)
 
         ww_d = keep.tile([P, 2 * H], U8, name="ww_d", align_bytes=64)
         ws_d = keep.tile([P, H], U8, name="ws_d", align_bytes=64)
-        nc.vector.tensor_copy(
-            ww_d[:].rearrange("p (t m b) -> p m t b", t=PACK, b=2), ww[:].rearrange("p (m t b) -> p m t b", t=PACK, b=2)
-        )
-        nc.vector.tensor_copy(
-            ws_d[:].rearrange("p (t m) -> p m t", t=PACK), ws[:].rearrange("p (m t) -> p m t", t=PACK)
-        )
 
+        def deal_words(tiles):
+            nc.vector.tensor_copy(
+                ww_d[:].rearrange("p (t m b) -> p m t b", t=PACK, b=2)[:, :, tiles, :],
+                ww[:].rearrange("p (m t b) -> p m t b", t=PACK, b=2)[:, :, tiles, :],
+            )
+
+        def deal_scales(tiles):
+            nc.vector.tensor_copy(
+                ws_d[:].rearrange("p (t m) -> p m t", t=PACK)[:, :, tiles],
+                ws[:].rearrange("p (m t) -> p m t", t=PACK)[:, :, tiles],
+            )
+
+        deal_words(slice(0, 1))
         xq_s = keep.tile([P, S], U8, name="xq_s", align_bytes=64)
         nc.vector.tensor_copy(xq_s[:], xs[:].indirect(offs_t[:]))
+        deal_scales(slice(0, 1))
         xq_w = keep.tile([P, S], U32, name="xq_w", align_bytes=64)
         for h in range(2):
             nc.vector.tensor_copy(
                 xq_w[:, h * HALF : (h + 1) * HALF],
                 xw[:].bitcast(U32).indirect(offs_t[:, h * HALF // 16 : (h + 1) * HALF // 16]),
             )
+        deal_words(slice(1, PACK))
+        deal_scales(slice(1, PACK))
 
         yg = keep.tile([P, PACK, S], F32, name="yg")
 
@@ -104,14 +110,12 @@ def tile_picked_candgvarpagez_none_po_kernel(
                 start=True,
                 stop=True,
             )
-            if t < SCALAR_SQUARES:
-                nc.scalar.activation(ysq[t][:, cols], y_ps[:], ACT.Square)
-                y_of.append((t, cols, y_ps))
-            else:
-                y_sb = ring.tile([P, n], F32, name="y_sb", bufs=PACK - SCALAR_SQUARES)
-                nc.vector.tensor_copy(y_sb[:], y_ps[:])
-                nc.vector.tensor_tensor(ysq[t][:, cols], y_ps[:], y_sb[:], ALU.mult)
-                y_of.append((t, cols, y_sb))
+            y_of.append((t, cols, y_ps))
+
+        def square(tile):
+            for t, cols, y in y_of:
+                if t == tile:
+                    nc.scalar.activation(ysq[t][:, cols], y[:], ACT.Square)
 
         def weigh(tiles):
             for t, cols, y in y_of:
@@ -149,10 +153,15 @@ def tile_picked_candgvarpagez_none_po_kernel(
         last = len(CHUNKS) - 1
         mb_of, qs_of, r_of, s_ps_of = {}, {}, {}, {}
 
+        def chunk_tile(c, t, shape, dtype, name):
+            if c == 0:
+                return keep.tile(shape, dtype, name=name + "_0", tag="page%d" % t, align_bytes=64)
+            return ring.tile(shape, dtype, name=name, align_bytes=64)
+
         def fetch(c, t):
             n = CHUNKS[c]
             if t == 0:
-                qs_of[c] = ring.tile([P, PACK, n], F32, name="qs")
+                qs_of[c] = chunk_tile(c, 0, [P, PACK, n], F32, "qs")
                 mb_of[c, 0] = ring.tile([P, n * MEMBERS], F32, name="mb_first", bufs=1)[:]
             if t == 1:
                 rest = ring.tile([P, PACK - 1, n * MEMBERS], F32, name="mb_rest", bufs=1)
@@ -164,20 +173,20 @@ def tile_picked_candgvarpagez_none_po_kernel(
             nc.vector.tensor_reduce(qs_of[c][:, t, :], mb.rearrange("p (j m) -> p j m", m=MEMBERS), AX.X, ALU.add)
 
         def root(c):
-            r_of[c] = ring.tile([P, PACK, CHUNKS[c]], F32, name="r")
+            r_of[c] = chunk_tile(c, 1, [P, PACK, CHUNKS[c]], F32, "r")
             nc.scalar.activation(r_of[c][:], qs_of[c][:], ACT.Abs_reciprocal_sqrt, bias=0.5)
 
         def score(c):
             n = CHUNKS[c]
             cols = slice(starts[c], starts[c] + n)
-            zb = ring.tile([P, n * PACK], BF16, name="zb", align_bytes=64)
+            zb = chunk_tile(c, 2, [P, n * PACK], BF16, "zb")
             nc.vector.tensor_tensor(
                 zb[:].rearrange("p (g i t) -> p g t i", i=4, t=PACK),
                 yg[:, :, cols].rearrange("p t (g i) -> p g t i", i=4),
                 r_of[c][:].rearrange("p t (g i) -> p g t i", i=4),
                 ALU.mult,
             )
-            z_w = ring.tile([P, n], U32, name="z_w", align_bytes=64)
+            z_w = chunk_tile(c, 3, [P, n], U32, "z_w")
             z_s = ring.tile([P, n], U8, name="z_s", align_bytes=64)
             nc.vector.quantize_mx(out=z_w[:].bitcast(FP8X4), scales=z_s[:], in_=zb[:])
             s_ps = psum.tile([P, PACK, n], F32, name="s_ps", bufs=2)
@@ -197,18 +206,28 @@ def tile_picked_candgvarpagez_none_po_kernel(
             cols = slice(starts[c], starts[c] + CHUNKS[c])
             nc.vector.tensor_scalar(s_sb[:, tiles, cols], s_ps_of[c][:, tiles, :], -0.0625, None, ALU.mult)
 
-        weigh((0, 1, 2, 3))
+        page = []
+        square(0)
         cand_words()
         fetch(0, 0)
-        cand_scales()
+        square(1)
+        weigh((0, 1))
         fetch(0, 1)
-        cand_deal()
+        square(2)
+        cand_scales()
         fetch(0, 2)
+        square(3)
+        weigh((2, 3))
         fetch(0, 3)
+        cand_deal()
         for c in range(1, len(CHUNKS)):
             fetch(c, 0)
             root(c - 1)
             score(c - 1)
+            if c == 1:
+                for t in range(PACK):
+                    page.append(keep.tile([P, U], F32, name="page%d" % t, tag="page%d" % t, align_bytes=64))
+                    nc.gpsimd.memset(page[t][:], 0.0)
             fetch(c, 1)
             copy_s(c - 1, slice(0, PACK))
             fetch(c, 2)

@@ -20,6 +20,9 @@ K, T, S, H, C, U = 512, 2048, 512, 512, 512, 1024
 MEMBERS = 4
 CHUNKS = [128, 128, 128, 64, 64]
 SPARE = 16
+FUSED = 2
+LATE = sum(CHUNKS[-2:])
+EARLY = S - LATE
 HALF = S // 2
 FLOPS = 2 * K * H * S + 2 * H * C * S
 
@@ -63,6 +66,10 @@ def tile_picked_candgvarpagez_none_po_kernel(
         nc.sync.dma_start(gs_t[:], gs.rearrange("(p t) o -> p (t o)", t=PACK))
         nc.sync.dma_start(n3_t[:], n3)
         nc.sync.dma_start(n2_t[:], n2)
+
+        warm = keep.tile([P, 2], F32, name="warm")
+        nc.gpsimd.memset(warm[:, 0:1], 1.0)
+        nc.scalar.activation(warm[:, 1:2], warm[:, 0:1], ACT.Abs_reciprocal_sqrt, bias=0.5)
 
         ysq = [keep.tile([P, S + SPARE], F32, name="ysq%d" % t) for t in range(PACK)]
         for t in range(PACK):
@@ -114,15 +121,23 @@ def tile_picked_candgvarpagez_none_po_kernel(
 
         def square(tile):
             for t, cols, y in y_of:
-                if t == tile:
+                if t == tile and t < 4:
                     nc.scalar.activation(ysq[t][:, cols], y[:], ACT.Square)
+                elif t == tile:
+                    y_sb = keep.tile([P, S], F32, name="y_sb%d" % t)
+                    nc.vector.tensor_copy(y_sb[:], y[:])
+                    nc.vector.tensor_tensor(ysq[t][:, cols], y[:], y_sb[:], ALU.mult)
+                    y_sb_of[t] = y_sb
 
         def weigh(tiles):
             for t, cols, y in y_of:
-                if t in tiles:
+                if t in tiles and t < 4:
                     nc.vector.tensor_scalar(yg[:, t, cols], y[:], gs_t[:, t : t + 1], None, ALU.mult)
+                elif t in tiles:
+                    nc.vector.tensor_scalar(yg[:, t, cols], y_sb_of[t][:], gs_t[:, t : t + 1], None, ALU.mult)
 
         y_of = []
+        y_sb_of = {}
         project(0, 0, HALF)
         project(0, HALF, HALF)
         for t in range(1, PACK):
@@ -154,15 +169,15 @@ def tile_picked_candgvarpagez_none_po_kernel(
         mb_of, qs_of, r_of, s_ps_of = {}, {}, {}, {}
 
         def chunk_tile(c, t, shape, dtype, name):
-            if c == 0:
-                return keep.tile(shape, dtype, name=name + "_0", tag="page%d" % t, align_bytes=64)
+            if c == 1:
+                return keep.tile(shape, dtype, name=name + "_1", tag="page%d" % t, align_bytes=64)
             return ring.tile(shape, dtype, name=name, align_bytes=64)
 
         def fetch(c, t):
             n = CHUNKS[c]
             if t == 0:
                 qs_of[c] = chunk_tile(c, 0, [P, PACK, n], F32, "qs")
-                mb_of[c, 0] = ring.tile([P, n * MEMBERS], F32, name="mb_first", bufs=1)[:]
+                mb_of[c, 0] = keep.tile([P, n * MEMBERS], F32, name="mb_first", tag="mb_first")[:]
             if t == 1:
                 rest = ring.tile([P, PACK - 1, n * MEMBERS], F32, name="mb_rest", bufs=1)
                 for u in range(1, PACK):
@@ -172,9 +187,12 @@ def tile_picked_candgvarpagez_none_po_kernel(
             nc.scalar.activation(mb, ysq[t][:].indirect(n1_t[:, lst]), ACT.Copy)
             nc.vector.tensor_reduce(qs_of[c][:, t, :], mb.rearrange("p (j m) -> p j m", m=MEMBERS), AX.X, ALU.add)
 
-        def root(c):
-            r_of[c] = chunk_tile(c, 1, [P, PACK, CHUNKS[c]], F32, "r")
-            nc.scalar.activation(r_of[c][:], qs_of[c][:], ACT.Abs_reciprocal_sqrt, bias=0.5)
+        def root(c, tiles):
+            if tiles.start == 0:
+                r_of[c] = chunk_tile(c, 1, [P, PACK, CHUNKS[c]], F32, "r")
+            nc.scalar.activation(r_of[c][:, tiles, :], qs_of[c][:, tiles, :], ACT.Abs_reciprocal_sqrt, bias=0.5)
+
+        late_ps = []
 
         def score(c):
             n = CHUNKS[c]
@@ -189,10 +207,21 @@ def tile_picked_candgvarpagez_none_po_kernel(
             z_w = chunk_tile(c, 3, [P, n], U32, "z_w")
             z_s = ring.tile([P, n], U8, name="z_s", align_bytes=64)
             nc.vector.quantize_mx(out=z_w[:].bitcast(FP8X4), scales=z_s[:], in_=zb[:])
-            s_ps = psum.tile([P, PACK, n], F32, name="s_ps", bufs=2)
+            if c < last - 1:
+                s_ps_of[c] = psum.tile([P, PACK, n], F32, name="s_ps", bufs=2)
+                outs = [s_ps_of[c][:, t, :] for t in range(PACK)]
+            else:
+                if c == last - 1:
+                    for t in range(FUSED):
+                        late_ps.append(psum.tile([P, LATE], F32, name="late_ps%d" % t, tag="y_ps%d_0" % t)[:])
+                    rest = psum.tile([P, PACK - FUSED, LATE], F32, name="late_rest", tag="y_ps%d_0" % FUSED)
+                    late_ps.append(rest[:])
+                part = slice(starts[c] - EARLY, starts[c] - EARLY + n)
+                outs = [late_ps[t][:, part] for t in range(FUSED)]
+                outs.extend(late_ps[FUSED][:, t, part] for t in range(PACK - FUSED))
             for t in range(PACK):
                 nc.tensor.matmul_mx(
-                    out=s_ps[:, t, :],
+                    out=outs[t],
                     lhsT=xc_wd[:, P * t : P * (t + 1)].bitcast(FP8X4),
                     lhsT_scale=xc_sd[:, P * t : P * (t + 1)],
                     rhs=z_w[:].bitcast(FP8X4),
@@ -200,47 +229,57 @@ def tile_picked_candgvarpagez_none_po_kernel(
                     start=True,
                     stop=True,
                 )
-            s_ps_of[c] = s_ps
 
-        def copy_s(c, tiles):
+        def copy_s(c):
             cols = slice(starts[c], starts[c] + CHUNKS[c])
-            nc.vector.tensor_scalar(s_sb[:, tiles, cols], s_ps_of[c][:, tiles, :], -0.0625, None, ALU.mult)
+            nc.vector.tensor_scalar(s_sb[:, :, cols], s_ps_of[c][:], -0.0625, None, ALU.mult)
 
         page = []
         square(0)
         cand_words()
+        weigh((0,))
         fetch(0, 0)
         square(1)
-        weigh((0, 1))
+        cand_scales()
         fetch(0, 1)
         square(2)
-        cand_scales()
+        weigh((1, 2))
         fetch(0, 2)
         square(3)
-        weigh((2, 3))
+        weigh((3,))
         fetch(0, 3)
         cand_deal()
         for c in range(1, len(CHUNKS)):
             fetch(c, 0)
-            root(c - 1)
+            root(c - 1, slice(0, PACK))
             score(c - 1)
-            if c == 1:
+            if c == 2:
                 for t in range(PACK):
                     page.append(keep.tile([P, U], F32, name="page%d" % t, tag="page%d" % t, align_bytes=64))
                     nc.gpsimd.memset(page[t][:], 0.0)
-            fetch(c, 1)
-            copy_s(c - 1, slice(0, PACK))
-            fetch(c, 2)
-            fetch(c, 3)
-        root(last)
+            for t in range(1, PACK):
+                fetch(c, t)
+            if c < last:
+                copy_s(c - 1)
+        root(last, slice(0, PACK - 1))
+        nrelu = [keep.tile([P, S], F32, name="nrelu%d" % t) for t in range(FUSED)]
+        nc.vector.tensor_scalar(nrelu[0][:, :EARLY], s_sb[:, 0, :EARLY], 0.0, None, ALU.min)
+        root(last, slice(PACK - 1, PACK))
         score(last)
-        copy_s(last, slice(0, 1))
+        nc.vector.tensor_scalar(nrelu[1][:, :EARLY], s_sb[:, 1, :EARLY], 0.0, None, ALU.min)
+
+        def finish_window(t):
+            nc.vector.tensor_scalar(nrelu[t][:, EARLY:], late_ps[t], -0.0625, 0.0, ALU.mult, ALU.min)
 
         out_rows = out_0.rearrange("(p t) u -> p t u", t=PACK)
 
         def put(t, j0, n, final=False):
-            nw = ring.tile([P, n], F32, name="nw", bufs=8)
+            nw = ring.tile([P, n], F32, name="nw", bufs=9)
             lst = slice(j0 // 16, (j0 + n) // 16)
+            if t < FUSED:
+                nc.vector.tensor_tensor(nw[:], nrelu[t][:].indirect(n3_t[:, lst]), s_sb[:, t, j0 : j0 + n], ALU.subtract)
+                nc.scalar.activation(page[t][:].indirect(n2_t[:, lst]), nw[:], ACT.Copy)
+                return
             if final:
                 got = keep.tile([P, n], F32, name="got_final", tag="rounded", align_bytes=64)
             else:
@@ -249,11 +288,16 @@ def tile_picked_candgvarpagez_none_po_kernel(
             nc.vector.scalar_tensor_tensor(nw[:], got[:], 0.0, s_sb[:, t, j0 : j0 + n], ALU.min, ALU.subtract)
             nc.scalar.activation(page[t][:].indirect(n2_t[:, lst]), nw[:], ACT.Copy)
 
+        finish_window(0)
         put(0, 0, 128)
-        copy_s(last, slice(1, PACK))
+        finish_window(1)
         put(1, 0, 256)
-        put(0, 128, 384)
+        put(0, 128, 256)
+        for t in range(FUSED):
+            nc.vector.tensor_scalar(s_sb[:, t, EARLY:], late_ps[t], -0.0625, None, ALU.mult)
+        nc.vector.tensor_scalar(s_sb[:, FUSED:, EARLY:], late_ps[FUSED], -0.0625, None, ALU.mult)
         put(1, 256, 256)
+        put(0, 384, 128)
         put(2, 0, 256)
         put(3, 0, 128)
         put(2, 256, 256)

from contextlib import ExitStack

import concourse.mybir as mybir

F32 = mybir.dt.float32
BF16 = mybir.dt.bfloat16
I32 = mybir.dt.int32
U32 = mybir.dt.uint32
U16 = mybir.dt.uint16
U8 = mybir.dt.uint8
FP8X4 = mybir.dt.float8_e4m3fn_x4
FP4X4 = mybir.dt.float4_e2m1fn_x4
ALU = mybir.AluOpType
ACT = mybir.ActivationFunctionType
AX = mybir.AxisListType

P = 128
PACK = 4
K, T, S, H, C, U = 512, 2048, 512, 512, 512, 1024
MEMBERS = 4
CHUNKS = [128, 128, 128, 64, 64]
SPARE = 16
FUSED = 2
LATE = sum(CHUNKS[-2:])
EARLY = S - LATE
HALF = S // 2
FLOPS = 2 * K * H * S + 2 * H * C * S


def tile_picked_candgvarpagez_none_po_kernel(
    tc, x_words, x_scales, w1_words, w1_scales, gs, offs, n1, cand, n2, n3, out_0, out_1, out_2
):
    nc = tc.nc
    with ExitStack() as ctx:
        keep = ctx.enter_context(tc.tile_pool(name="keep", bufs=1))
        ring = ctx.enter_context(tc.tile_pool(name="ring", bufs=2))
        psum = ctx.enter_context(tc.psum_pool(name="psum", bufs=1))

        offs_t = keep.tile([P, S // 16], U16, name="offs_t")
        n1_t = keep.tile([P, S * MEMBERS // 16], U16, name="n1_t")
        cand_t = keep.tile([P, C // 16], U16, name="cand_t")
        n2_t = keep.tile([P, S // 16], U16, name="n2_t")
        n3_t = keep.tile([P, S // 16], U16, name="n3_t")

        xw = keep.tile([P, T], I32, name="xw", align_bytes=64)
        xs = keep.tile([P, T], U8, name="xs", align_bytes=64)
        ww = keep.tile([P, 2 * H], U8, name="ww", align_bytes=64)
        ws = keep.tile([P, H], U8, name="ws", align_bytes=64)
        gs_t = keep.tile([P, PACK], F32, name="gs_t")

        nc.vector.memset(xs[:].bitcast(I32), 0)
        nc.gpsimd.memset(ws[:].bitcast(I32), 0)

        def load_scale_rows(engine, tile, scales, q):
            engine.dma_start(tile[32 * q : 32 * q + 4, :].bitcast(I32), scales[0, 4 * q : 4 * q + 4, :].bitcast(I32))

        nc.sync.dma_start(offs_t[:], offs)
        nc.sync.dma_start(xw[:], x_words[0].rearrange("p c r -> p (c r)").bitcast(I32))
        nc.scalar.dma_start(ww[:].bitcast(I32), w1_words[0].bitcast(I32))
        for q in range(4):
            load_scale_rows(nc.scalar, xs, x_scales, q)
        for q in range(4):
            load_scale_rows(nc.scalar if q < 2 else nc.gpsimd, ws, w1_scales, q)
        nc.sync.dma_start(n1_t[:], n1)
        nc.sync.dma_start(cand_t[:], cand)
        nc.sync.dma_start(gs_t[:], gs.rearrange("(p t) o -> p (t o)", t=PACK))
        nc.sync.dma_start(n3_t[:], n3)
        nc.sync.dma_start(n2_t[:], n2)

        warm = keep.tile([P, 2], F32, name="warm")
        nc.gpsimd.memset(warm[:, 0:1], 1.0)
        nc.scalar.activation(warm[:, 1:2], warm[:, 0:1], ACT.Abs_reciprocal_sqrt, bias=0.5)

        ysq = [keep.tile([P, S + SPARE], F32, name="ysq%d" % t) for t in range(PACK)]
        for t in range(PACK):
            nc.gpsimd.memset(ysq[t][:, S:], 0.0)

        ww_d = keep.tile([P, 2 * H], U8, name="ww_d", align_bytes=64)
        ws_d = keep.tile([P, H], U8, name="ws_d", align_bytes=64)

        def deal_words(tiles):
            nc.vector.tensor_copy(
                ww_d[:].rearrange("p (t m b) -> p m t b", t=PACK, b=2)[:, :, tiles, :],
                ww[:].rearrange("p (m t b) -> p m t b", t=PACK, b=2)[:, :, tiles, :],
            )

        def deal_scales(tiles):
            nc.vector.tensor_copy(
                ws_d[:].rearrange("p (t m) -> p m t", t=PACK)[:, :, tiles],
                ws[:].rearrange("p (m t) -> p m t", t=PACK)[:, :, tiles],
            )

        deal_words(slice(0, 1))
        xq_s = keep.tile([P, S], U8, name="xq_s", align_bytes=64)
        nc.vector.tensor_copy(xq_s[:], xs[:].indirect(offs_t[:]))
        deal_scales(slice(0, 1))
        xq_w = keep.tile([P, S], U32, name="xq_w", align_bytes=64)
        for h in range(2):
            nc.vector.tensor_copy(
                xq_w[:, h * HALF : (h + 1) * HALF],
                xw[:].bitcast(U32).indirect(offs_t[:, h * HALF // 16 : (h + 1) * HALF // 16]),
            )
        deal_words(slice(1, PACK))
        deal_scales(slice(1, PACK))

        yg = keep.tile([P, PACK, S], F32, name="yg")

        def project(t, j0, n):
            cols = slice(j0, j0 + n)
            y_ps = psum.tile([P, n], F32, name="y_ps%d_%d" % (t, j0))
            nc.tensor.matmul_mx(
                out=y_ps[:],
                lhsT=ww_d[:, 2 * P * t : 2 * P * (t + 1)].bitcast(FP4X4),
                lhsT_scale=ws_d[:, P * t : P * (t + 1)],
                rhs=xq_w[:, cols].bitcast(FP8X4),
                rhs_scale=xq_s[:, cols],
                start=True,
                stop=True,
            )
            y_of.append((t, cols, y_ps))

        def square(tile):
            for t, cols, y in y_of:
                if t == tile and t < 4:
                    nc.scalar.activation(ysq[t][:, cols], y[:], ACT.Square)
                elif t == tile:
                    y_sb = keep.tile([P, S], F32, name="y_sb%d" % t)
                    nc.vector.tensor_copy(y_sb[:], y[:])
                    nc.vector.tensor_tensor(ysq[t][:, cols], y[:], y_sb[:], ALU.mult)
                    y_sb_of[t] = y_sb

        def weigh(tiles):
            for t, cols, y in y_of:
                if t in tiles and t < 4:
                    nc.vector.tensor_scalar(yg[:, t, cols], y[:], gs_t[:, t : t + 1], None, ALU.mult)
                elif t in tiles:
                    nc.vector.tensor_scalar(yg[:, t, cols], y_sb_of[t][:], gs_t[:, t : t + 1], None, ALU.mult)

        y_of = []
        y_sb_of = {}
        project(0, 0, HALF)
        project(0, HALF, HALF)
        for t in range(1, PACK):
            project(t, 0, S)

        xc_w = keep.tile([P, C], U32, name="xc_w", align_bytes=64)
        xc_s = keep.tile([P, C], U8, name="xc_s", align_bytes=64)
        xc_wd = keep.tile([P, C], U32, name="xc_wd", align_bytes=64)
        xc_sd = keep.tile([P, C], U8, name="xc_sd", align_bytes=64)

        def cand_words():
            nc.vector.tensor_copy(xc_w[:], xw[:].bitcast(U32).indirect(cand_t[:]))

        def cand_scales():
            nc.vector.tensor_copy(xc_s[:], xs[:].indirect(cand_t[:]))

        def cand_deal():
            nc.vector.tensor_copy(
                xc_wd[:].bitcast(I32).rearrange("p (t m) -> p t m", t=PACK),
                xc_w[:].bitcast(I32).rearrange("p (m t) -> p t m", t=PACK),
            )
            nc.vector.tensor_copy(
                xc_sd[:].rearrange("p (t m) -> p m t", t=PACK), xc_s[:].rearrange("p (m t) -> p m t", t=PACK)
            )

        s_sb = keep.tile([P, PACK, S], F32, name="s_sb")
        starts = [sum(CHUNKS[:c]) for c in range(len(CHUNKS))]
        last = len(CHUNKS) - 1
        mb_of, qs_of, r_of, s_ps_of = {}, {}, {}, {}

        def chunk_tile(c, t, shape, dtype, name):
            if c == 1:
                return keep.tile(shape, dtype, name=name + "_1", tag="page%d" % t, align_bytes=64)
            return ring.tile(shape, dtype, name=name, align_bytes=64)

        def fetch(c, t):
            n = CHUNKS[c]
            if t == 0:
                qs_of[c] = chunk_tile(c, 0, [P, PACK, n], F32, "qs")
                mb_of[c, 0] = keep.tile([P, n * MEMBERS], F32, name="mb_first", tag="mb_first")[:]
            if t == 1:
                rest = ring.tile([P, PACK - 1, n * MEMBERS], F32, name="mb_rest", bufs=1)
                for u in range(1, PACK):
                    mb_of[c, u] = rest[:, u - 1, :]
            mb = mb_of[c, t]
            lst = slice(starts[c] * MEMBERS // 16, (starts[c] + n) * MEMBERS // 16)
            nc.scalar.activation(mb, ysq[t][:].indirect(n1_t[:, lst]), ACT.Copy)
            nc.vector.tensor_reduce(qs_of[c][:, t, :], mb.rearrange("p (j m) -> p j m", m=MEMBERS), AX.X, ALU.add)

        def root(c, tiles):
            if tiles.start == 0:
                r_of[c] = chunk_tile(c, 1, [P, PACK, CHUNKS[c]], F32, "r")
            nc.scalar.activation(r_of[c][:, tiles, :], qs_of[c][:, tiles, :], ACT.Abs_reciprocal_sqrt, bias=0.5)

        late_ps = []

        def score(c):
            n = CHUNKS[c]
            cols = slice(starts[c], starts[c] + n)
            zb = chunk_tile(c, 2, [P, n * PACK], BF16, "zb")
            nc.vector.tensor_tensor(
                zb[:].rearrange("p (g i t) -> p g t i", i=4, t=PACK),
                yg[:, :, cols].rearrange("p t (g i) -> p g t i", i=4),
                r_of[c][:].rearrange("p t (g i) -> p g t i", i=4),
                ALU.mult,
            )
            z_w = chunk_tile(c, 3, [P, n], U32, "z_w")
            z_s = ring.tile([P, n], U8, name="z_s", align_bytes=64)
            nc.vector.quantize_mx(out=z_w[:].bitcast(FP8X4), scales=z_s[:], in_=zb[:])
            if c < last - 1:
                s_ps_of[c] = psum.tile([P, PACK, n], F32, name="s_ps", bufs=2)
                outs = [s_ps_of[c][:, t, :] for t in range(PACK)]
            else:
                if c == last - 1:
                    for t in range(FUSED):
                        late_ps.append(psum.tile([P, LATE], F32, name="late_ps%d" % t, tag="y_ps%d_0" % t)[:])
                    rest = psum.tile([P, PACK - FUSED, LATE], F32, name="late_rest", tag="y_ps%d_0" % FUSED)
                    late_ps.append(rest[:])
                part = slice(starts[c] - EARLY, starts[c] - EARLY + n)
                outs = [late_ps[t][:, part] for t in range(FUSED)]
                outs.extend(late_ps[FUSED][:, t, part] for t in range(PACK - FUSED))
            for t in range(PACK):
                nc.tensor.matmul_mx(
                    out=outs[t],
                    lhsT=xc_wd[:, P * t : P * (t + 1)].bitcast(FP8X4),
                    lhsT_scale=xc_sd[:, P * t : P * (t + 1)],
                    rhs=z_w[:].bitcast(FP8X4),
                    rhs_scale=z_s[:],
                    start=True,
                    stop=True,
                )

        def copy_s(c):
            cols = slice(starts[c], starts[c] + CHUNKS[c])
            nc.vector.tensor_scalar(s_sb[:, :, cols], s_ps_of[c][:], -0.0625, None, ALU.mult)

        page = []
        square(0)
        cand_words()
        weigh((0,))
        fetch(0, 0)
        square(1)
        cand_scales()
        fetch(0, 1)
        square(2)
        weigh((1, 2))
        fetch(0, 2)
        square(3)
        weigh((3,))
        fetch(0, 3)
        cand_deal()
        for c in range(1, len(CHUNKS)):
            fetch(c, 0)
            root(c - 1, slice(0, PACK))
            score(c - 1)
            if c == 2:
                for t in range(PACK):
                    page.append(keep.tile([P, U], F32, name="page%d" % t, tag="page%d" % t, align_bytes=64))
                    nc.gpsimd.memset(page[t][:], 0.0)
            for t in range(1, PACK):
                fetch(c, t)
            if c < last:
                copy_s(c - 1)
        root(last, slice(0, PACK - 1))
        nrelu = [keep.tile([P, S], F32, name="nrelu%d" % t) for t in range(FUSED)]
        nc.vector.tensor_scalar(nrelu[0][:, :EARLY], s_sb[:, 0, :EARLY], 0.0, None, ALU.min)
        root(last, slice(PACK - 1, PACK))
        score(last)
        nc.vector.tensor_scalar(nrelu[1][:, :EARLY], s_sb[:, 1, :EARLY], 0.0, None, ALU.min)

        def finish_window(t):
            nc.vector.tensor_scalar(nrelu[t][:, EARLY:], late_ps[t], -0.0625, 0.0, ALU.mult, ALU.min)

        out_rows = out_0.rearrange("(p t) u -> p t u", t=PACK)

        def put(t, j0, n, final=False):
            nw = ring.tile([P, n], F32, name="nw", bufs=9)
            lst = slice(j0 // 16, (j0 + n) // 16)
            if t < FUSED:
                nc.vector.tensor_tensor(nw[:], nrelu[t][:].indirect(n3_t[:, lst]), s_sb[:, t, j0 : j0 + n], ALU.subtract)
                nc.scalar.activation(page[t][:].indirect(n2_t[:, lst]), nw[:], ACT.Copy)
                return
            if final:
                got = keep.tile([P, n], F32, name="got_final", tag="rounded", align_bytes=64)
            else:
                got = ring.tile([P, n], F32, name="got", bufs=3)
            nc.vector.tensor_copy(got[:], s_sb[:, t, :].indirect(n3_t[:, lst]))
            nc.vector.scalar_tensor_tensor(nw[:], got[:], 0.0, s_sb[:, t, j0 : j0 + n], ALU.min, ALU.subtract)
            nc.scalar.activation(page[t][:].indirect(n2_t[:, lst]), nw[:], ACT.Copy)

        finish_window(0)
        put(0, 0, 128)
        finish_window(1)
        put(1, 0, 256)
        put(0, 128, 256)
        for t in range(FUSED):
            nc.vector.tensor_scalar(s_sb[:, t, EARLY:], late_ps[t], -0.0625, None, ALU.mult)
        nc.vector.tensor_scalar(s_sb[:, FUSED:, EARLY:], late_ps[FUSED], -0.0625, None, ALU.mult)
        put(1, 256, 256)
        put(0, 384, 128)
        put(2, 0, 256)
        put(3, 0, 128)
        put(2, 256, 256)
        put(3, 128, 384, final=True)

        rounded = keep.tile([P, U * PACK], BF16, name="rounded", tag="rounded", align_bytes=64)

        def round_page(t, h):
            cols = slice(h * U // 2, (h + 1) * U // 2)
            nc.vector.tensor_copy(rounded[:].rearrange("p (u t) -> p u t", t=PACK)[:, cols, t], page[t][:, cols])

        for t in range(PACK):
            nc.sync.dma_start(out_rows[:, t, :], page[t][:])
            if t < PACK - 1:
                round_page(t, 0)
                round_page(t, 1)

        o_w = keep.tile([P, U], U32, name="o_w", align_bytes=64)
        o_s = keep.tile([P, U], U8, name="o_s", align_bytes=64)
        words_out = out_1[0].rearrange("p c r -> p (c r)").bitcast(I32)
        for h in range(2):
            round_page(PACK - 1, h)
        for h in range(2):
            cols = slice(h * U // 2, (h + 1) * U // 2)
            nc.vector.quantize_mx(
                out=o_w[:, cols].bitcast(FP8X4), scales=o_s[:, cols], in_=rounded[:, h * 2 * U : (h + 1) * 2 * U]
            )
            nc.sync.dma_start(words_out[:, cols], o_w[:, cols].bitcast(I32))
        for q in range(4):
            (nc.scalar if q < 3 else nc.sync).dma_start(
                out_2[0, 4 * q : 4 * q + 4, :].bitcast(I32), o_s[32 * q : 32 * q + 4, :].bitcast(I32)
            )
